import numpy as np
import ml_dtypes


def mxq(x, axis, fmt="e4m3"):
    dtype, down = {"e4m3": (ml_dtypes.float8_e4m3fn, 7), "e5m2": (ml_dtypes.float8_e5m2, 14)}[fmt]
    v = np.moveaxis(np.asarray(x, np.float32).astype(ml_dtypes.bfloat16).astype(np.float64), axis, -1)
    blocks = v.reshape(v.shape[:-1] + (-1, 32))
    amax = np.abs(blocks).max(-1, keepdims=True)
    byte = np.maximum(np.where(amax > 0, np.frexp(amax)[1] - 1 + 127, 0) - down, 1)
    scale = np.exp2(byte - 127.0)
    codes = (blocks / scale).astype(np.float32).astype(dtype).astype(np.float64)
    return np.moveaxis((codes * scale).reshape(v.shape), -1, axis)


WIDE = False


def mx_kscale(k):
    if not WIDE:
        return np.ones(k)
    levels = np.array([10, -10, 5, -5, 0])
    if k % 512:
        return np.exp2(np.random.permutation(np.resize(levels, k // 32))).repeat(32)
    a = np.empty((k // 512, 16))
    for p in range(k // 512):
        a[p, :8] = np.random.permutation(np.resize(levels, 8))
        for g in range(8):
            far = levels[np.abs(levels - a[p, g]) >= 10]
            a[p, g + 8] = far[np.random.randint(len(far))]
    return np.exp2(a.ravel()).repeat(32)


def f64(x):
    return np.asarray(x).astype(np.float64)


def striped8(idx):
    return np.asarray(idx).reshape(8, -1, 16).transpose(0, 2, 1).reshape(128, -1).astype(np.uint16)


def unstriped8(offs):
    return offs.reshape(8, 16, -1).transpose(0, 2, 1).reshape(8, -1).astype(np.int64)


def pick8(x, idx, run):
    r = np.arange(len(x))
    return x[r[:, None], idx[r % (8 * run) // run]]


E2M1 = np.array([0.0, 0.5, 1.0, 1.5, 2.0, 3.0, 4.0, 6.0, -0.0, -0.5, -1.0, -1.5, -2.0, -3.0, -4.0, -6.0])


def pack_weight(w, fmt):
    k, n = w.shape
    w = f64(np.asarray(w, np.float32).astype(ml_dtypes.bfloat16)).reshape(k // 32, 32, n)
    amax = np.abs(w).max(1)
    if fmt == "e4m3":
        byte = np.frexp(amax)[1] - 1 + 127 - 7
    else:
        mant, ex = np.frexp(amax / 6.0)
        byte = np.where(mant > 0.5, ex, ex - 1) + 127
    byte = np.clip(np.where(amax > 0, byte, 1), 1, 254)
    scaled = (w * np.exp2(127.0 - byte)[:, None, :]).reshape(k, n).astype(np.float32)
    by_word = np.ascontiguousarray(scaled.reshape(k // 512, 128, 4, n).transpose(0, 1, 3, 2))
    if fmt == "e4m3":
        words = by_word.astype(ml_dtypes.float8_e4m3fn).view(np.uint8)
    else:
        c = by_word.astype(ml_dtypes.float4_e2m1fn).view(np.uint8) & 0xF
        words = (c[..., 0::2] | (c[..., 1::2] << 4)).reshape(k // 512, 128, 2 * n)
    return np.ascontiguousarray(words), np.ascontiguousarray(byte.astype(np.uint8).reshape(k // 512, 16, n))


def unpack_weight(words, scales, fmt):
    g, _, n = scales.shape
    words = np.ascontiguousarray(words).reshape(g, 128, n, -1)
    if fmt == "e4m3":
        vals = words.view(ml_dtypes.float8_e4m3fn).astype(np.float64)
    else:
        nib = np.empty((g, 128, n, 4), np.uint8)
        nib[..., 0::2] = words & 0xF
        nib[..., 1::2] = words >> 4
        vals = E2M1[nib]
    vals = vals * np.repeat(np.exp2(scales.astype(np.float64) - 127.0), 8, axis=1)[..., None]
    return vals.transpose(0, 1, 3, 2).reshape(g * 512, n)


def softplus(v):
    return np.log(1.0 + np.exp(v))


D, T, I, Q = 512, 1024, 512, 128


def setup_inputs():
    n = np.random.standard_normal
    idx = np.stack([np.random.permutation(T)[:I] for _ in range(8)])
    idx2 = np.stack([np.random.permutation(T)[:I] for _ in range(8)])
    idx3 = np.stack([np.random.permutation(T)[:I] for _ in range(8)])
    fd = mx_kscale(D)
    keysp = pack_weight(n((D, T)) / fd[:, None], "e2m1")
    return {
        "query": (n((D, Q)) * 0.9 / np.sqrt(D) * fd[:, None]).astype(np.float32),
        "query2": (n((D, Q)) * 0.9 / np.sqrt(D) * fd[:, None]).astype(np.float32),
        "keys_words": keysp[0],
        "keys_scales": keysp[1],
        "lam": (np.random.uniform(0.6, 1.2, (Q, 1))).astype(np.float32),
        "old": (1.0 * n((Q, T))).astype(np.float32),
        "share2": (np.random.uniform(0.4, 1.2, (Q, 1))).astype(np.float32),
        "offs": striped8(idx),
        "offs2": striped8(idx2),
        "offs3": striped8(idx3),
    }


def reference(query, query2, keys_words, keys_scales, lam, old, share2, offs, offs2, offs3):
    idx = unstriped8(offs)
    idx2 = unstriped8(offs2)
    idx3 = unstriped8(offs3)
    keysu = unpack_weight(keys_words, keys_scales, "e2m1")
    queryq = mxq(f64(query), 0, "e4m3")
    a = queryq.T @ keysu
    query2q = mxq(f64(query2), 0, "e4m3")
    b = query2q.T @ keysu
    w = pick8(a, idx, 16) / (softplus(pick8(b, idx2, 16)) + 0.5) * f64(lam)
    f1 = np.zeros((Q, T))
    f1[np.arange(Q)[:, None], idx[np.arange(Q) % 128 // 16]] = w
    f2 = np.zeros((Q, T))
    f2[np.arange(Q)[:, None], idx3[np.arange(Q) % 128 // 16]] = w
    y = f64(old) + f1 + f2 * f64(share2)
    return y

@@ -1,0 +1,182 @@
+from contextlib import ExitStack
+
+import concourse.mybir as mybir
+from concourse.masks import make_identity
+
+D, T, I, Q = 512, 1024, 512, 128
+FLOPS = 2 * 2 * D * T * Q
+
+F32 = mybir.dt.float32
+BF16 = mybir.dt.bfloat16
+I32 = mybir.dt.int32
+U32 = mybir.dt.uint32
+U16 = mybir.dt.uint16
+U8 = mybir.dt.uint8
+FP8X4 = mybir.dt.float8_e4m3fn_x4
+FP4X4 = mybir.dt.float4_e2m1fn_x4
+ACT = mybir.ActivationFunctionType
+ALU = mybir.AluOpType
+
+P = 128
+PACK = 4
+GROUP = 16
+EXP_CAP = 2.0**60
+B_COLS = 256
+A_COLS = 512
+HALF = I // 2
+FIRST = 128
+STORE_COLS = 256
+BANK = 512
+
+
+def tile_attend_worthfor_lean_twiceput_heads_kernel(
+    tc, query, query2, keys_words, keys_scales, lam, old, share2, offs, offs2, offs3, out
+):
+    nc = tc.nc
+    with ExitStack() as ctx:
+        sb = ctx.enter_context(tc.tile_pool(name="sb", bufs=1))
+        ps = ctx.enter_context(tc.psum_pool(name="ps", bufs=1))
+
+        list1 = sb.tile([P, I // GROUP], U16, name="list1")
+        list2 = sb.tile([P, I // GROUP], U16, name="list2")
+        list3 = sb.tile([P, I // GROUP], U16, name="list3")
+
+        def entries(tile, lo, hi):
+            return tile[:, lo // GROUP : hi // GROUP]
+
+        raw2 = sb.tile([P, PACK, Q], F32, name="raw2")
+        raw1 = sb.tile([P, PACK, Q], F32, name="raw1")
+        words = sb.tile([P, 2 * T], U8, name="words", align_bytes=64)
+        plane = sb.tile([P, T], U8, name="plane", align_bytes=64)
+        lam_col = sb.tile([P, 1], F32, name="lam_col")
+        share_col = sb.tile([P, 1], F32, name="share_col")
+        old_sb = sb.tile([P, T], F32, name="old_sb")
+        f1 = sb.tile([P, T], F32, name="f1")
+        f2 = sb.tile([P, T], F32, name="f2")
+        one = sb.tile([P, 1], F32, name="one")
+        half = sb.tile([P, 1], F32, name="half")
+
+        nc.vector.memset(plane[:].bitcast(I32), 0)
+        nc.vector.memset(one[:], 1.0)
+        nc.sync.dma_start(out=raw2[:], in_=query2.rearrange("(p j) q -> p j q", j=PACK))
+        nc.sync.dma_start(out=words[:].bitcast(I32), in_=keys_words[0].bitcast(I32))
+        for quad in range(4):
+            nc.scalar.dma_start(
+                out=plane[32 * quad : 32 * quad + 4, :].bitcast(I32),
+                in_=keys_scales[0, 4 * quad : 4 * quad + 4, :].bitcast(I32),
+            )
+        nc.sync.dma_start(out=raw1[:], in_=query.rearrange("(p j) q -> p j q", j=PACK))
+        nc.sync.dma_start(list2[:], offs2)
+        nc.sync.dma_start(list1[:], offs)
+        nc.sync.dma_start(out=lam_col[:], in_=lam)
+        nc.sync.dma_start(out=old_sb[:], in_=old)
+        nc.sync.dma_start(list3[:], offs3)
+        nc.sync.dma_start(out=share_col[:], in_=share2)
+
+        nc.scalar.activation(half[:], one[:], ACT.Copy, scale=0.5)
+        nc.vector.memset(f1[:], 0.0)
+        nc.vector.memset(f2[:], 0.0)
+
+        def quantise(raw, cast, name):
+            grouped = sb.tile([P, Q, PACK], BF16, name=name + "_grouped", align_bytes=64)
+            codes = sb.tile([P, Q], U32, name=name + "_codes", align_bytes=64)
+            scales = sb.tile([P, Q], U8, name=name + "_scales", align_bytes=64)
+            cast(
+                grouped[:].rearrange("p (c i) t -> p c t i", i=4),
+                raw[:].rearrange("p t (c i) -> p c t i", i=4),
+            )
+            nc.vector.quantize_mx(
+                out=codes[:].bitcast(FP8X4),
+                scales=scales[:],
+                in_=grouped[:].rearrange("p q t -> p (q t)"),
+            )
+            return codes, scales
+
+        def scores(codes, scales, lo, hi, name):
+            bank = ps.tile([P, hi - lo], F32, name=name, tag=name)
+            nc.tensor.matmul_mx(
+                out=bank[:],
+                lhsT=codes[:].bitcast(FP8X4),
+                lhsT_scale=scales[:],
+                rhs=words[:, 2 * lo : 2 * hi].bitcast(FP4X4),
+                rhs_scale=plane[:, lo:hi],
+                start=True,
+                stop=True,
+            )
+            return bank
+
+        codes2, scales2 = quantise(raw2, nc.vector.tensor_copy, "q2")
+        codes1, scales1 = quantise(raw1, nc.scalar.copy, "q1")
+
+        b_sb = sb.tile([P, T], F32, name="b_sb")
+        for n, lo in enumerate(range(0, T, B_COLS)):
+            bank = scores(codes2, scales2, lo, lo + B_COLS, "b_bank%d" % n)
+            copy = nc.vector.tensor_copy if n % 2 == 0 else nc.scalar.copy
+            copy(b_sb[:, lo : lo + B_COLS], bank[:])
+        a_banks = [scores(codes1, scales1, lo, lo + A_COLS, "a_bank%d" % lo) for lo in range(0, T, A_COLS)]
+
+        gb = sb.tile([P, I], F32, name="gb")
+        e = sb.tile([P, I], F32, name="e")
+        nc.vector.tensor_copy(gb[:, HALF:], b_sb[:].indirect(entries(list2, HALF, I)))
+        nc.scalar.activation(e[:, :HALF], b_sb[:].indirect(entries(list2, 0, HALF)), ACT.Exp)
+        nc.scalar.activation(e[:, HALF:], gb[:, HALF:], ACT.Exp)
+        nc.vector.tensor_copy(gb[:, :HALF], b_sb[:].indirect(entries(list2, 0, HALF)))
+        capped = sb.tile([P, I], F32, name="capped")
+        nc.vector.tensor_scalar(capped[:], e[:], EXP_CAP, None, ALU.min)
+
+        a_sb = sb.tile([P, T], F32, name="a_sb")
+        for n, bank in enumerate(a_banks):
+            nc.vector.tensor_copy(a_sb[:, n * A_COLS : (n + 1) * A_COLS], bank[:])
+
+        lg = sb.tile([P, I], F32, name="lg")
+        sp = sb.tile([P, I], F32, name="sp")
+        nc.scalar.activation(lg[:], capped[:], ACT.Ln, bias=one[:])
+        nc.vector.tensor_tensor(sp[:], lg[:], gb[:], ALU.max)
+
+        ga = sb.tile([P, I], F32, name="ga")
+        num = sb.tile([P, I], F32, name="num")
+        nc.vector.tensor_copy(ga[:], a_sb[:].indirect(list1[:]))
+        nc.vector.tensor_scalar(num[:], ga[:], lam_col[:], None, ALU.mult)
+
+        ident = sb.tile([P, P], F32, name="ident")
+        make_identity(nc, ident[:])
+        turned = [ps.tile([P, BANK], F32, name="turned%d" % n) for n in range(T // BANK)]
+
+        def turn_into(bank, src, first, last):
+            for j in range(BANK // P):
+                nc.tensor.matmul(
+                    bank[:, j * P : (j + 1) * P],
+                    src[:, j * P : (j + 1) * P],
+                    ident[:],
+                    is_transpose=True,
+                    start=first and j == 0,
+                    stop=last and j == BANK // P - 1,
+                )
+
+        for n, bank in enumerate(turned):
+            turn_into(bank, old_sb[:, n * BANK : (n + 1) * BANK], True, False)
+
+        rs = sb.tile([P, I], F32, name="rs")
+        r = sb.tile([P, I], F32, name="r")
+        for lo, hi in ((0, FIRST), (FIRST, HALF), (HALF, I)):
+            nc.scalar.activation(rs[:, lo:hi], sp[:, lo:hi], ACT.Abs_reciprocal_sqrt, bias=half[:])
+            nc.scalar.activation(r[:, lo:hi], rs[:, lo:hi], ACT.Square)
+        for lo, hi in ((0, FIRST), (FIRST, I)):
+            nc.vector.tensor_tensor(f1[:].indirect(entries(list1, lo, hi)), num[:, lo:hi], r[:, lo:hi], ALU.mult)
+        nc.vector.tensor_tensor(f2[:].indirect(list3[:]), num[:], r[:], ALU.mult)
+
+        part_t = sb.tile([P, T], F32, name="part_t")
+        total = sb.tile([P, T], F32, name="total")
+        for n, bank in enumerate(turned):
+            turn_into(bank, f1[:, n * BANK : (n + 1) * BANK], False, True)
+            nc.scalar.copy(part_t[:, n * BANK : (n + 1) * BANK], bank[:])
+        for n in range(T // BANK):
+            part = ps.tile([P, BANK], F32, name="part%d" % n, tag="a_bank%d" % (n * A_COLS))
+            turn_into(part, part_t[:, n * BANK : (n + 1) * BANK], True, True)
+            for k, lo in enumerate(range(0, BANK, STORE_COLS)):
+                cols = slice(n * BANK + lo, n * BANK + lo + STORE_COLS)
+                nc.vector.scalar_tensor_tensor(
+                    total[:, cols], f2[:, cols], share_col[:], part[:, lo : lo + STORE_COLS], ALU.mult, ALU.add
+                )
+                queue = nc.sync if k % 2 == 0 else nc.scalar
+                queue.dma_start(out=out[:, cols], in_=total[:, cols])

@@ -54,14 +54,14 @@ def tile_attend_worthfor_lean_twiceput_heads_kernel(
         f1 = sb.tile([P, T], F32, name="f1")
         f2 = sb.tile([P, T], F32, name="f2")
         one = sb.tile([P, 1], F32, name="one")
-        half = sb.tile([P, 1], F32, name="half")
+        quarter = sb.tile([P, 1], F32, name="quarter")
 
-        nc.vector.memset(plane[:].bitcast(I32), 0)
+        nc.gpsimd.memset(plane[:].bitcast(I32), 0)
         nc.vector.memset(one[:], 1.0)
         nc.sync.dma_start(out=raw2[:], in_=query2.rearrange("(p j) q -> p j q", j=PACK))
         nc.sync.dma_start(out=words[:].bitcast(I32), in_=keys_words[0].bitcast(I32))
         for quad in range(4):
-            nc.scalar.dma_start(
+            nc.sync.dma_start(
                 out=plane[32 * quad : 32 * quad + 4, :].bitcast(I32),
                 in_=keys_scales[0, 4 * quad : 4 * quad + 4, :].bitcast(I32),
             )
@@ -73,23 +73,25 @@ def tile_attend_worthfor_lean_twiceput_heads_kernel(
         nc.sync.dma_start(list3[:], offs3)
         nc.sync.dma_start(out=share_col[:], in_=share2)
 
-        nc.scalar.activation(half[:], one[:], ACT.Copy, scale=0.5)
+        nc.scalar.activation(quarter[:], one[:], ACT.Copy, scale=0.25)
         nc.vector.memset(f1[:], 0.0)
         nc.vector.memset(f2[:], 0.0)
 
-        def quantise(raw, cast, name):
+        def quantise(raw, casts, piece, name):
             grouped = sb.tile([P, Q, PACK], BF16, name=name + "_grouped", align_bytes=64)
             codes = sb.tile([P, Q], U32, name=name + "_codes", align_bytes=64)
             scales = sb.tile([P, Q], U8, name=name + "_scales", align_bytes=64)
-            cast(
-                grouped[:].rearrange("p (c i) t -> p c t i", i=4),
-                raw[:].rearrange("p t (c i) -> p c t i", i=4),
-            )
-            nc.vector.quantize_mx(
-                out=codes[:].bitcast(FP8X4),
-                scales=scales[:],
-                in_=grouped[:].rearrange("p q t -> p (q t)"),
-            )
+            for cast, lo in zip(casts, range(0, Q, Q // 2)):
+                cast(
+                    grouped[:, lo : lo + Q // 2, :].rearrange("p (c i) t -> p c t i", i=4),
+                    raw[:, :, lo : lo + Q // 2].rearrange("p t (c i) -> p c t i", i=4),
+                )
+            for lo in range(0, Q, piece):
+                nc.vector.quantize_mx(
+                    out=codes[:, lo : lo + piece].bitcast(FP8X4),
+                    scales=scales[:, lo : lo + piece],
+                    in_=grouped[:, lo : lo + piece, :].rearrange("p q t -> p (q t)"),
+                )
             return codes, scales
 
         def scores(codes, scales, lo, hi, name):
@@ -105,8 +107,8 @@ def tile_attend_worthfor_lean_twiceput_heads_kernel(
             )
             return bank
 
-        codes2, scales2 = quantise(raw2, nc.vector.tensor_copy, "q2")
-        codes1, scales1 = quantise(raw1, nc.scalar.copy, "q1")
+        codes2, scales2 = quantise(raw2, (nc.vector.tensor_copy, nc.vector.tensor_copy), Q // 2, "q2")
+        codes1, scales1 = quantise(raw1, (nc.vector.tensor_copy, nc.scalar.copy), Q, "q1")
 
         b_sb = sb.tile([P, T], F32, name="b_sb")
         for n, lo in enumerate(range(0, T, B_COLS)):
@@ -131,7 +133,13 @@ def tile_attend_worthfor_lean_twiceput_heads_kernel(
         lg = sb.tile([P, I], F32, name="lg")
         sp = sb.tile([P, I], F32, name="sp")
         nc.scalar.activation(lg[:], capped[:], ACT.Ln, bias=one[:])
-        nc.vector.tensor_tensor(sp[:], lg[:], gb[:], ALU.max)
+        sq = sb.tile([P, I], F32, name="sq")
+        for lo in (0, HALF):
+            cols = slice(lo, lo + HALF)
+            nc.vector.tensor_tensor(sp[:, cols], lg[:, cols], gb[:, cols], ALU.max)
+        for lo in (0, HALF):
+            cols = slice(lo, lo + HALF)
+            nc.vector.scalar_tensor_tensor(sq[:, cols], sp[:, cols], 1.0, sp[:, cols], ALU.add, ALU.mult)
 
         ga = sb.tile([P, I], F32, name="ga")
         num = sb.tile([P, I], F32, name="num")
@@ -140,43 +148,40 @@ def tile_attend_worthfor_lean_twiceput_heads_kernel(
 
         ident = sb.tile([P, P], F32, name="ident")
         make_identity(nc, ident[:])
-        turned = [ps.tile([P, BANK], F32, name="turned%d" % n) for n in range(T // BANK)]
+        units = range(0, T, B_COLS)
+        turned = [ps.tile([P, B_COLS], F32, name="turned%d" % n, tag="b_bank%d" % n) for n in range(len(units))]
 
         def turn_into(bank, src, first, last):
-            for j in range(BANK // P):
+            for j in range(B_COLS // P):
                 nc.tensor.matmul(
                     bank[:, j * P : (j + 1) * P],
                     src[:, j * P : (j + 1) * P],
                     ident[:],
                     is_transpose=True,
                     start=first and j == 0,
-                    stop=last and j == BANK // P - 1,
+                    stop=last and j == B_COLS // P - 1,
                 )
 
-        for n, bank in enumerate(turned):
-            turn_into(bank, old_sb[:, n * BANK : (n + 1) * BANK], True, False)
+        for bank, lo in zip(turned, units):
+            turn_into(bank, old_sb[:, lo : lo + B_COLS], True, False)
 
-        rs = sb.tile([P, I], F32, name="rs")
         r = sb.tile([P, I], F32, name="r")
-        for lo, hi in ((0, FIRST), (FIRST, HALF), (HALF, I)):
-            nc.scalar.activation(rs[:, lo:hi], sp[:, lo:hi], ACT.Abs_reciprocal_sqrt, bias=half[:])
-            nc.scalar.activation(r[:, lo:hi], rs[:, lo:hi], ACT.Square)
         for lo, hi in ((0, FIRST), (FIRST, I)):
-            nc.vector.tensor_tensor(f1[:].indirect(entries(list1, lo, hi)), num[:, lo:hi], r[:, lo:hi], ALU.mult)
-        nc.vector.tensor_tensor(f2[:].indirect(list3[:]), num[:], r[:], ALU.mult)
+            nc.scalar.activation(r[:, lo:hi], sq[:, lo:hi], ACT.Abs_reciprocal_sqrt, bias=quarter[:])
+        nc.vector.tensor_tensor(f2[:].indirect(entries(list3, 0, FIRST)), num[:, :FIRST], r[:, :FIRST], ALU.mult)
+        nc.vector.tensor_tensor(f1[:].indirect(list1[:]), num[:], r[:], ALU.mult)
+        nc.vector.tensor_tensor(f2[:].indirect(entries(list3, FIRST, I)), num[:, FIRST:], r[:, FIRST:], ALU.mult)
 
         part_t = sb.tile([P, T], F32, name="part_t")
         total = sb.tile([P, T], F32, name="total")
-        for n, bank in enumerate(turned):
-            turn_into(bank, f1[:, n * BANK : (n + 1) * BANK], False, True)
-            nc.scalar.copy(part_t[:, n * BANK : (n + 1) * BANK], bank[:])
-        for n in range(T // BANK):
-            part = ps.tile([P, BANK], F32, name="part%d" % n, tag="a_bank%d" % (n * A_COLS))
-            turn_into(part, part_t[:, n * BANK : (n + 1) * BANK], True, True)
-            for k, lo in enumerate(range(0, BANK, STORE_COLS)):
-                cols = slice(n * BANK + lo, n * BANK + lo + STORE_COLS)
-                nc.vector.scalar_tensor_tensor(
-                    total[:, cols], f2[:, cols], share_col[:], part[:, lo : lo + STORE_COLS], ALU.mult, ALU.add
-                )
-                queue = nc.sync if k % 2 == 0 else nc.scalar
-                queue.dma_start(out=out[:, cols], in_=total[:, cols])
+        for bank, lo in zip(turned, units):
+            turn_into(bank, f1[:, lo : lo + B_COLS], False, True)
+            nc.scalar.copy(part_t[:, lo : lo + B_COLS], bank[:])
+        part_tags = ["a_bank0", "a_bank%d" % A_COLS, "part2", "part3"]
+        for n, lo in enumerate(units):
+            cols = slice(lo, lo + B_COLS)
+            part = ps.tile([P, B_COLS], F32, name="part%d" % n, tag=part_tags[n])
+            turn_into(part, part_t[:, cols], True, True)
+            nc.vector.scalar_tensor_tensor(total[:, cols], f2[:, cols], share_col[:], part[:], ALU.mult, ALU.add)
+            queue = nc.sync if n % 2 == 0 else nc.scalar
+            queue.dma_start(out=out[:, cols], in_=total[:, cols])

from contextlib import ExitStack

import concourse.mybir as mybir
from concourse.masks import make_identity

D, T, I, Q = 512, 1024, 512, 128
FLOPS = 2 * 2 * D * T * Q

F32 = mybir.dt.float32
BF16 = mybir.dt.bfloat16
I32 = mybir.dt.int32
U32 = mybir.dt.uint32
U16 = mybir.dt.uint16
U8 = mybir.dt.uint8
FP8X4 = mybir.dt.float8_e4m3fn_x4
FP4X4 = mybir.dt.float4_e2m1fn_x4
ACT = mybir.ActivationFunctionType
ALU = mybir.AluOpType

P = 128
PACK = 4
GROUP = 16
EXP_CAP = 2.0**60
B_COLS = 256
A_COLS = 512
HALF = I // 2
FIRST = 128
STORE_COLS = 256
BANK = 512


def tile_attend_worthfor_lean_twiceput_heads_kernel(
    tc, query, query2, keys_words, keys_scales, lam, old, share2, offs, offs2, offs3, out
):
    nc = tc.nc
    with ExitStack() as ctx:
        sb = ctx.enter_context(tc.tile_pool(name="sb", bufs=1))
        ps = ctx.enter_context(tc.psum_pool(name="ps", bufs=1))

        list1 = sb.tile([P, I // GROUP], U16, name="list1")
        list2 = sb.tile([P, I // GROUP], U16, name="list2")
        list3 = sb.tile([P, I // GROUP], U16, name="list3")

        def entries(tile, lo, hi):
            return tile[:, lo // GROUP : hi // GROUP]

        raw2 = sb.tile([P, PACK, Q], F32, name="raw2")
        raw1 = sb.tile([P, PACK, Q], F32, name="raw1")
        words = sb.tile([P, 2 * T], U8, name="words", align_bytes=64)
        plane = sb.tile([P, T], U8, name="plane", align_bytes=64)
        lam_col = sb.tile([P, 1], F32, name="lam_col")
        share_col = sb.tile([P, 1], F32, name="share_col")
        old_sb = sb.tile([P, T], F32, name="old_sb")
        f1 = sb.tile([P, T], F32, name="f1")
        f2 = sb.tile([P, T], F32, name="f2")
        one = sb.tile([P, 1], F32, name="one")
        quarter = sb.tile([P, 1], F32, name="quarter")

        nc.gpsimd.memset(plane[:].bitcast(I32), 0)
        nc.vector.memset(one[:], 1.0)
        nc.sync.dma_start(out=raw2[:], in_=query2.rearrange("(p j) q -> p j q", j=PACK))
        nc.sync.dma_start(out=words[:].bitcast(I32), in_=keys_words[0].bitcast(I32))
        for quad in range(4):
            nc.sync.dma_start(
                out=plane[32 * quad : 32 * quad + 4, :].bitcast(I32),
                in_=keys_scales[0, 4 * quad : 4 * quad + 4, :].bitcast(I32),
            )
        nc.sync.dma_start(out=raw1[:], in_=query.rearrange("(p j) q -> p j q", j=PACK))
        nc.sync.dma_start(list2[:], offs2)
        nc.sync.dma_start(list1[:], offs)
        nc.sync.dma_start(out=lam_col[:], in_=lam)
        nc.sync.dma_start(out=old_sb[:], in_=old)
        nc.sync.dma_start(list3[:], offs3)
        nc.sync.dma_start(out=share_col[:], in_=share2)

        nc.scalar.activation(quarter[:], one[:], ACT.Copy, scale=0.25)
        nc.vector.memset(f1[:], 0.0)
        nc.vector.memset(f2[:], 0.0)

        def quantise(raw, casts, piece, name):
            grouped = sb.tile([P, Q, PACK], BF16, name=name + "_grouped", align_bytes=64)
            codes = sb.tile([P, Q], U32, name=name + "_codes", align_bytes=64)
            scales = sb.tile([P, Q], U8, name=name + "_scales", align_bytes=64)
            for cast, lo in zip(casts, range(0, Q, Q // 2)):
                cast(
                    grouped[:, lo : lo + Q // 2, :].rearrange("p (c i) t -> p c t i", i=4),
                    raw[:, :, lo : lo + Q // 2].rearrange("p t (c i) -> p c t i", i=4),
                )
            for lo in range(0, Q, piece):
                nc.vector.quantize_mx(
                    out=codes[:, lo : lo + piece].bitcast(FP8X4),
                    scales=scales[:, lo : lo + piece],
                    in_=grouped[:, lo : lo + piece, :].rearrange("p q t -> p (q t)"),
                )
            return codes, scales

        def scores(codes, scales, lo, hi, name):
            bank = ps.tile([P, hi - lo], F32, name=name, tag=name)
            nc.tensor.matmul_mx(
                out=bank[:],
                lhsT=codes[:].bitcast(FP8X4),
                lhsT_scale=scales[:],
                rhs=words[:, 2 * lo : 2 * hi].bitcast(FP4X4),
                rhs_scale=plane[:, lo:hi],
                start=True,
                stop=True,
            )
            return bank

        codes2, scales2 = quantise(raw2, (nc.vector.tensor_copy, nc.vector.tensor_copy), Q // 2, "q2")
        codes1, scales1 = quantise(raw1, (nc.vector.tensor_copy, nc.scalar.copy), Q, "q1")

        b_sb = sb.tile([P, T], F32, name="b_sb")
        for n, lo in enumerate(range(0, T, B_COLS)):
            bank = scores(codes2, scales2, lo, lo + B_COLS, "b_bank%d" % n)
            copy = nc.vector.tensor_copy if n % 2 == 0 else nc.scalar.copy
            copy(b_sb[:, lo : lo + B_COLS], bank[:])
        a_banks = [scores(codes1, scales1, lo, lo + A_COLS, "a_bank%d" % lo) for lo in range(0, T, A_COLS)]

        gb = sb.tile([P, I], F32, name="gb")
        e = sb.tile([P, I], F32, name="e")
        nc.vector.tensor_copy(gb[:, HALF:], b_sb[:].indirect(entries(list2, HALF, I)))
        nc.scalar.activation(e[:, :HALF], b_sb[:].indirect(entries(list2, 0, HALF)), ACT.Exp)
        nc.scalar.activation(e[:, HALF:], gb[:, HALF:], ACT.Exp)
        nc.vector.tensor_copy(gb[:, :HALF], b_sb[:].indirect(entries(list2, 0, HALF)))
        capped = sb.tile([P, I], F32, name="capped")
        nc.vector.tensor_scalar(capped[:], e[:], EXP_CAP, None, ALU.min)

        a_sb = sb.tile([P, T], F32, name="a_sb")
        for n, bank in enumerate(a_banks):
            nc.vector.tensor_copy(a_sb[:, n * A_COLS : (n + 1) * A_COLS], bank[:])

        lg = sb.tile([P, I], F32, name="lg")
        sp = sb.tile([P, I], F32, name="sp")
        nc.scalar.activation(lg[:], capped[:], ACT.Ln, bias=one[:])
        sq = sb.tile([P, I], F32, name="sq")
        for lo in (0, HALF):
            cols = slice(lo, lo + HALF)
            nc.vector.tensor_tensor(sp[:, cols], lg[:, cols], gb[:, cols], ALU.max)
        for lo in (0, HALF):
            cols = slice(lo, lo + HALF)
            nc.vector.scalar_tensor_tensor(sq[:, cols], sp[:, cols], 1.0, sp[:, cols], ALU.add, ALU.mult)

        ga = sb.tile([P, I], F32, name="ga")
        num = sb.tile([P, I], F32, name="num")
        nc.vector.tensor_copy(ga[:], a_sb[:].indirect(list1[:]))
        nc.vector.tensor_scalar(num[:], ga[:], lam_col[:], None, ALU.mult)

        ident = sb.tile([P, P], F32, name="ident")
        make_identity(nc, ident[:])
        units = range(0, T, B_COLS)
        turned = [ps.tile([P, B_COLS], F32, name="turned%d" % n, tag="b_bank%d" % n) for n in range(len(units))]

        def turn_into(bank, src, first, last):
            for j in range(B_COLS // P):
                nc.tensor.matmul(
                    bank[:, j * P : (j + 1) * P],
                    src[:, j * P : (j + 1) * P],
                    ident[:],
                    is_transpose=True,
                    start=first and j == 0,
                    stop=last and j == B_COLS // P - 1,
                )

        for bank, lo in zip(turned, units):
            turn_into(bank, old_sb[:, lo : lo + B_COLS], True, False)

        r = sb.tile([P, I], F32, name="r")
        for lo, hi in ((0, FIRST), (FIRST, I)):
            nc.scalar.activation(r[:, lo:hi], sq[:, lo:hi], ACT.Abs_reciprocal_sqrt, bias=quarter[:])
        nc.vector.tensor_tensor(f2[:].indirect(entries(list3, 0, FIRST)), num[:, :FIRST], r[:, :FIRST], ALU.mult)
        nc.vector.tensor_tensor(f1[:].indirect(list1[:]), num[:], r[:], ALU.mult)
        nc.vector.tensor_tensor(f2[:].indirect(entries(list3, FIRST, I)), num[:, FIRST:], r[:, FIRST:], ALU.mult)

        part_t = sb.tile([P, T], F32, name="part_t")
        total = sb.tile([P, T], F32, name="total")
        for bank, lo in zip(turned, units):
            turn_into(bank, f1[:, lo : lo + B_COLS], False, True)
            nc.scalar.copy(part_t[:, lo : lo + B_COLS], bank[:])
        part_tags = ["a_bank0", "a_bank%d" % A_COLS, "part2", "part3"]
        for n, lo in enumerate(units):
            cols = slice(lo, lo + B_COLS)
            part = ps.tile([P, B_COLS], F32, name="part%d" % n, tag=part_tags[n])
            turn_into(part, part_t[:, cols], True, True)
            nc.vector.scalar_tensor_tensor(total[:, cols], f2[:, cols], share_col[:], part[:], ALU.mult, ALU.add)
            queue = nc.sync if n % 2 == 0 else nc.scalar
            queue.dma_start(out=out[:, cols], in_=total[:, cols])
